import numpy as np
import ml_dtypes


def mxq(x, axis, fmt="e4m3"):
    dtype, down = {"e4m3": (ml_dtypes.float8_e4m3fn, 7), "e5m2": (ml_dtypes.float8_e5m2, 14)}[fmt]
    v = np.moveaxis(np.asarray(x, np.float32).astype(ml_dtypes.bfloat16).astype(np.float64), axis, -1)
    blocks = v.reshape(v.shape[:-1] + (-1, 32))
    amax = np.abs(blocks).max(-1, keepdims=True)
    byte = np.maximum(np.where(amax > 0, np.frexp(amax)[1] - 1 + 127, 0) - down, 1)
    scale = np.exp2(byte - 127.0)
    codes = (blocks / scale).astype(np.float32).astype(dtype).astype(np.float64)
    return np.moveaxis((codes * scale).reshape(v.shape), -1, axis)


WIDE = False


def mx_kscale(k):
    if not WIDE:
        return np.ones(k)
    levels = np.array([10, -10, 5, -5, 0])
    if k % 512:
        return np.exp2(np.random.permutation(np.resize(levels, k // 32))).repeat(32)
    a = np.empty((k // 512, 16))
    for p in range(k // 512):
        a[p, :8] = np.random.permutation(np.resize(levels, 8))
        for g in range(8):
            far = levels[np.abs(levels - a[p, g]) >= 10]
            a[p, g + 8] = far[np.random.randint(len(far))]
    return np.exp2(a.ravel()).repeat(32)


def f64(x):
    return np.asarray(x).astype(np.float64)


def striped(idx):
    return np.tile(idx.reshape(-1, 16).T, (8, 1)).astype(np.uint16)


def unstriped(offs):
    return offs[:16].T.reshape(-1).astype(np.int64)


K, T, S, V, H, N = 512, 2048, 512, 128, 512, 128


def setup_inputs():
    n = np.random.standard_normal
    s = mx_kscale(K)[:, None]
    u = mx_kscale(H)
    return {
        "xT": (n((K, T)) * s).astype(np.float32),
        "w1": (n((K, H)) / np.sqrt(K) / s * u).astype(np.float32),
        "w2": (n((H, N)) / np.sqrt(2 * H) / u[:, None]).astype(np.float32),
        "w3": (n((H, N)) / np.sqrt(2 * H) / u[:, None]).astype(np.float32),
        "offs": striped(np.random.permutation(T)[:S]),
    }


def reference(xT, w1, w2, w3, offs):
    xq = mxq(f64(xT)[:, unstriped(offs)], 0, "e4m3")
    h = mxq(f64(w1), 0, "e4m3").T @ xq
    mean = (h[:, :V] + h[:, V:2 * V] + h[:, 2 * V:3 * V] + h[:, 3 * V:4 * V]) / 4
    dev = np.sqrt(((h[:, :V] - mean) ** 2 + (h[:, V:2 * V] - mean) ** 2 + (h[:, 2 * V:3 * V] - mean) ** 2 + (h[:, 3 * V:4 * V] - mean) ** 2) / 4)
    return mxq(f64(w2), 0, "e4m3").T @ mxq(mean, 0, "e4m3") + mxq(f64(w3), 0, "e4m3").T @ mxq(dev, 0, "e4m3")

@@ -1,0 +1,156 @@
+from contextlib import ExitStack
+
+import concourse.mybir as mybir
+
+K, T, S, V, H, N = 512, 2048, 512, 128, 512, 128
+FLOPS = 2 * K * H * S + 2 * 2 * H * N * V
+
+F32 = mybir.dt.float32
+BF16 = mybir.dt.bfloat16
+U32 = mybir.dt.uint32
+U16 = mybir.dt.uint16
+U8 = mybir.dt.uint8
+FP8X4 = mybir.dt.float8_e4m3fn_x4
+ACT = mybir.ActivationFunctionType
+ALU = mybir.AluOpType
+
+P = 128
+PACK = 4
+HALF = S // 2
+MH = P // 2
+
+
+def tile_picked_statpool_none_e_kernel(tc, xT, w1, w2, w3, offs, out):
+    nc = tc.nc
+    with ExitStack() as ctx:
+        keep = ctx.enter_context(tc.tile_pool(name="keep", bufs=1))
+        psum = ctx.enter_context(tc.psum_pool(name="psum", bufs=1))
+
+        offsets = keep.tile([P, S // 16], U16, name="offsets")
+        x_rows = xT.rearrange("(p j) t -> p j t", j=PACK)
+        x_raw = [keep.tile([P, T], F32, name=f"x_raw{j}") for j in range(PACK)]
+        nc.sync.dma_start(out=x_raw[0][:], in_=x_rows[:, 0, :])
+        nc.sync.dma_start(offsets[:], offs)
+        for j in range(1, PACK):
+            nc.sync.dma_start(out=x_raw[j][:], in_=x_rows[:, j, :])
+        w1_rows = w1.rearrange("(p j) c -> p j c", j=PACK)
+        w1_raw = [keep.tile([P, PACK, H // 2], F32, name=f"w1_raw{h}") for h in range(2)]
+        for h in range(2):
+            nc.sync.dma_start(out=w1_raw[h][:], in_=w1_rows[:, :, h * (H // 2):(h + 1) * (H // 2)])
+        w23_raw = [keep.tile([P, PACK, N], F32, name=f"w23_raw{g}") for g in range(2)]
+        for g, w in enumerate((w2, w3)):
+            nc.sync.dma_start(out=w23_raw[g][:], in_=w.rearrange("(p j) n -> p j n", j=PACK))
+
+        zero = keep.tile([P, 1], F32, name="zero")
+        nc.gpsimd.memset(zero[:], 0.0)
+        zero_root = keep.tile([P, 1], F32, name="zero_root")
+        nc.scalar.activation(zero_root[:], zero[:], ACT.Sqrt)
+
+        x_bf = keep.tile([P, S, PACK], BF16, name="x_bf", align_bytes=64)
+        for j in range(PACK):
+            nc.vector.tensor_copy(x_bf[:, :, j], x_raw[j][:].indirect(offsets[:]))
+        x_codes = keep.tile([P, S], U32, name="x_codes", align_bytes=64)
+        x_scales = keep.tile([P, S], U8, name="x_scales", align_bytes=64)
+        nc.vector.quantize_mx(out=x_codes[:].bitcast(FP8X4), scales=x_scales[:],
+                              in_=x_bf[:].rearrange("p s j -> p (s j)"))
+
+        w1_codes = keep.tile([P, PACK, P], U32, name="w1_codes", align_bytes=64)
+        w1_scales = keep.tile([P, PACK, P], U8, name="w1_scales", align_bytes=64)
+        w1_bf = [[keep.tile([P, 2, MH, PACK], BF16, name=f"w1_bf{h}{tp}", align_bytes=64) for tp in range(2)]
+                 for h in range(2)]
+
+        def cast_w1(h, tp, on_vector):
+            src = w1_raw[h][:].rearrange("p j (m t) -> p m j t", t=PACK)[:, :, :, 2 * tp:2 * tp + 2]
+            dst = w1_bf[h][tp][:].rearrange("p t m j -> p m j t")
+            if on_vector:
+                nc.vector.tensor_copy(dst, src)
+            else:
+                nc.scalar.copy(dst, src)
+
+        def quant_w1(h, t):
+            cols = slice(h * MH, (h + 1) * MH)
+            nc.vector.quantize_mx(out=w1_codes[:, t, cols].bitcast(FP8X4), scales=w1_scales[:, t, cols],
+                                  in_=w1_bf[h][t // 2][:, t % 2, :, :].rearrange("p m j -> p (m j)"))
+
+        cast_w1(0, 0, False)
+        cast_w1(0, 1, False)
+        quant_w1(0, 0)
+        quant_w1(0, 1)
+        cast_w1(1, 0, True)
+        cast_w1(1, 1, False)
+        quant_w1(0, 2)
+        quant_w1(0, 3)
+        for t in range(PACK):
+            quant_w1(1, t)
+
+        w23_bf = keep.tile([P, 2, N, PACK], BF16, name="w23_bf", align_bytes=64)
+        for g in range(2):
+            nc.gpsimd.tensor_scalar(
+                w23_bf[:, g, :, :].rearrange("p (c i) j -> p c j i", i=4),
+                w23_raw[g][:].rearrange("p j (c i) -> p c j i", i=4),
+                1.0, 0.0, ALU.mult, ALU.add)
+        w23_codes = keep.tile([P, 2 * N], U32, name="w23_codes", align_bytes=64)
+        w23_scales = keep.tile([P, 2 * N], U8, name="w23_scales", align_bytes=64)
+
+        sums = keep.tile([P, PACK, 2, V], F32, name="sums")
+        diffs = keep.tile([P, PACK, 2, V], F32, name="diffs")
+        diffs_sq = keep.tile([P, PACK, 2, V], F32, name="diffs_sq")
+        late = [keep.tile([P, HALF], F32, name=f"late{t}") for t in range(PACK)]
+        for t in range(PACK):
+            banks = []
+            for half in (1, 0):
+                bank = psum.tile([P, HALF], F32, name=f"h{half}{t}", tag=f"h{half}{t}")
+                cols = slice(half * HALF, (half + 1) * HALF)
+                nc.tensor.matmul_mx(out=bank[:], lhsT=w1_codes[:, t, :].bitcast(FP8X4), lhsT_scale=w1_scales[:, t, :],
+                                    rhs=x_codes[:, cols].bitcast(FP8X4), rhs_scale=x_scales[:, cols],
+                                    start=True, stop=True)
+                banks.append(bank)
+            nc.scalar.activation(late[t][:], banks[0][:], ACT.Copy, scale=0.25)
+            nc.vector.scalar_tensor_tensor(sums[:, t, :, :].rearrange("p d v -> p (d v)"), banks[1][:], 0.25, late[t][:],
+                                           ALU.mult, ALU.add)
+            nc.vector.scalar_tensor_tensor(diffs[:, t, :, :].rearrange("p d v -> p (d v)"), banks[1][:], 0.25, late[t][:],
+                                           ALU.mult, ALU.subtract)
+            if t % 2 == 1:
+                nc.scalar.activation(diffs_sq[:, t - 1:t + 1, :, :], diffs[:, t - 1:t + 1, :, :], ACT.Square,
+                                     bias=zero_root[:])
+
+        cross = keep.tile([P, PACK, V], F32, name="cross")
+        nc.vector.tensor_tensor(cross[:], sums[:, :, 0, :], sums[:, :, 1, :], ALU.subtract)
+        cross_sq = keep.tile([P, PACK, V], F32, name="cross_sq")
+        nc.scalar.activation(cross_sq[:], cross[:], ACT.Square)
+
+        mean_bf = keep.tile([P, V, PACK], BF16, name="mean_bf", align_bytes=64)
+        nc.vector.tensor_tensor(mean_bf[:].rearrange("p (c i) t -> p c t i", i=4),
+                                sums[:, :, 0, :].rearrange("p t (c i) -> p c t i", i=4),
+                                sums[:, :, 1, :].rearrange("p t (c i) -> p c t i", i=4), ALU.add)
+        within = keep.tile([P, PACK, V], F32, name="within")
+        nc.vector.tensor_tensor(within[:], diffs_sq[:, :, 0, :], diffs_sq[:, :, 1, :], ALU.add)
+        nc.vector.quantize_mx(out=w23_codes[:].bitcast(FP8X4), scales=w23_scales[:],
+                              in_=w23_bf[:].rearrange("p g n j -> p (g n j)"))
+        stat_codes = [keep.tile([P, V], U32, name=f"stat_codes{g}", align_bytes=64) for g in range(2)]
+        stat_scales = [keep.tile([P, V], U8, name=f"stat_scales{g}", align_bytes=64) for g in range(2)]
+
+        VH = V // 2
+        var = [keep.tile([P, PACK, VH], F32, name=f"var{u}") for u in range(2)]
+        dev_bf = [keep.tile([P, VH, PACK], BF16, name=f"dev_bf{u}", align_bytes=64) for u in range(2)]
+        for u in range(2):
+            cols = slice(u * VH, (u + 1) * VH)
+            nc.vector.scalar_tensor_tensor(var[u][:], within[:, :, cols], 2.0, cross_sq[:, :, cols], ALU.mult, ALU.add)
+            nc.scalar.activation(dev_bf[u][:].rearrange("p (c i) t -> p c t i", i=4),
+                                 var[u][:].rearrange("p t (c i) -> p c t i", i=4), ACT.Sqrt)
+        nc.vector.quantize_mx(out=stat_codes[0][:].bitcast(FP8X4), scales=stat_scales[0][:],
+                              in_=mean_bf[:].rearrange("p v t -> p (v t)"))
+        for u in range(2):
+            cols = slice(u * VH, (u + 1) * VH)
+            nc.vector.quantize_mx(out=stat_codes[1][:, cols].bitcast(FP8X4), scales=stat_scales[1][:, cols],
+                                  in_=dev_bf[u][:].rearrange("p v t -> p (v t)"))
+
+        acc = psum.tile([P, V], F32, name="acc", tag="h10")
+        for g in range(2):
+            cols = slice(g * N, (g + 1) * N)
+            nc.tensor.matmul_mx(out=acc[:], lhsT=w23_codes[:, cols].bitcast(FP8X4), lhsT_scale=w23_scales[:, cols],
+                                rhs=stat_codes[g][:].bitcast(FP8X4), rhs_scale=stat_scales[g][:],
+                                start=(g == 0), stop=(g == 1))
+        result = keep.tile([P, V], F32, name="result")
+        nc.vector.tensor_copy(result[:], acc[:])
+        nc.sync.dma_start(out=out, in_=result[:])

@@ -46,17 +46,20 @@ def tile_picked_statpool_none_e_kernel(tc, xT, w1, w2, w3, offs, out):
         zero_root = keep.tile([P, 1], F32, name="zero_root")
         nc.scalar.activation(zero_root[:], zero[:], ACT.Sqrt)
 
-        x_bf = keep.tile([P, S, PACK], BF16, name="x_bf", align_bytes=64)
+        x_bf = [keep.tile([P, HALF, PACK], BF16, name=f"x_bf{h}", align_bytes=64) for h in range(2)]
         for j in range(PACK):
-            nc.vector.tensor_copy(x_bf[:, :, j], x_raw[j][:].indirect(offsets[:]))
-        x_codes = keep.tile([P, S], U32, name="x_codes", align_bytes=64)
-        x_scales = keep.tile([P, S], U8, name="x_scales", align_bytes=64)
-        nc.vector.quantize_mx(out=x_codes[:].bitcast(FP8X4), scales=x_scales[:],
-                              in_=x_bf[:].rearrange("p s j -> p (s j)"))
+            for half in (1, 0):
+                nc.vector.tensor_copy(x_bf[half][:, :, j],
+                                      x_raw[j][:].indirect(offsets[:, half * (HALF // 16):(half + 1) * (HALF // 16)]))
+        x_codes = [keep.tile([P, HALF], U32, name=f"x_codes{h}", align_bytes=64) for h in range(2)]
+        x_scales = [keep.tile([P, HALF], U8, name=f"x_scales{h}", align_bytes=64) for h in range(2)]
+        for half in (1, 0):
+            nc.vector.quantize_mx(out=x_codes[half][:].bitcast(FP8X4), scales=x_scales[half][:],
+                                  in_=x_bf[half][:].rearrange("p s j -> p (s j)"))
 
-        w1_codes = keep.tile([P, PACK, P], U32, name="w1_codes", align_bytes=64)
-        w1_scales = keep.tile([P, PACK, P], U8, name="w1_scales", align_bytes=64)
-        w1_bf = [[keep.tile([P, 2, MH, PACK], BF16, name=f"w1_bf{h}{tp}", align_bytes=64) for tp in range(2)]
+        w1_codes = [keep.tile([P, P], U32, name=f"w1_codes{t}", align_bytes=64) for t in range(PACK)]
+        w1_scales = [keep.tile([P, P], U8, name=f"w1_scales{t}", align_bytes=64) for t in range(PACK)]
+        w1_bf = [[keep.tile([P, 2, MH, PACK], BF16, name=f"w1_bf{h}{tp}", tag=f"w1_bf{h}{tp}", align_bytes=64) for tp in range(2)]
                  for h in range(2)]
 
         def cast_w1(h, tp, on_vector):
@@ -69,88 +72,122 @@ def tile_picked_statpool_none_e_kernel(tc, xT, w1, w2, w3, offs, out):
 
         def quant_w1(h, t):
             cols = slice(h * MH, (h + 1) * MH)
-            nc.vector.quantize_mx(out=w1_codes[:, t, cols].bitcast(FP8X4), scales=w1_scales[:, t, cols],
+            nc.vector.quantize_mx(out=w1_codes[t][:, cols].bitcast(FP8X4), scales=w1_scales[t][:, cols],
                                   in_=w1_bf[h][t // 2][:, t % 2, :, :].rearrange("p m j -> p (m j)"))
 
         cast_w1(0, 0, False)
         cast_w1(0, 1, False)
         quant_w1(0, 0)
         quant_w1(0, 1)
-        cast_w1(1, 0, True)
-        cast_w1(1, 1, False)
         quant_w1(0, 2)
         quant_w1(0, 3)
+        cast_w1(1, 0, False)
+        cast_w1(1, 1, False)
         for t in range(PACK):
             quant_w1(1, t)
 
-        w23_bf = keep.tile([P, 2, N, PACK], BF16, name="w23_bf", align_bytes=64)
-        for g in range(2):
-            nc.gpsimd.tensor_scalar(
-                w23_bf[:, g, :, :].rearrange("p (c i) j -> p c j i", i=4),
-                w23_raw[g][:].rearrange("p j (c i) -> p c j i", i=4),
-                1.0, 0.0, ALU.mult, ALU.add)
-        w23_codes = keep.tile([P, 2 * N], U32, name="w23_codes", align_bytes=64)
-        w23_scales = keep.tile([P, 2 * N], U8, name="w23_scales", align_bytes=64)
+        w23_codes = [keep.tile([P, N], U32, name=f"w23_codes{g}", align_bytes=64) for g in range(2)]
+        w23_scales = [keep.tile([P, N], U8, name=f"w23_scales{g}", align_bytes=64) for g in range(2)]
+        w2_bf = keep.tile([P, N, PACK], BF16, name="w2_bf", tag="w1_bf10", align_bytes=64)
+        nc.vector.tensor_copy(w2_bf[:].rearrange("p (c i) j -> p c j i", i=4),
+                              w23_raw[0][:].rearrange("p j (c i) -> p c j i", i=4))
+        nc.vector.quantize_mx(out=w23_codes[0][:].bitcast(FP8X4), scales=w23_scales[0][:],
+                              in_=w2_bf[:].rearrange("p n j -> p (n j)"))
 
+        VH = V // 2
         sums = keep.tile([P, PACK, 2, V], F32, name="sums")
-        diffs = keep.tile([P, PACK, 2, V], F32, name="diffs")
-        diffs_sq = keep.tile([P, PACK, 2, V], F32, name="diffs_sq")
+        diffs = [keep.tile([P, 2, V], F32, name=f"diffs{t}") for t in range(PACK)]
+        diffs_sq = [keep.tile([P, 2, V], F32, name=f"diffs_sq{t}") for t in range(PACK)]
         late = [keep.tile([P, HALF], F32, name=f"late{t}") for t in range(PACK)]
-        for t in range(PACK):
+        cross = [keep.tile([P, V], F32, name=f"cross{t}") for t in range(PACK)]
+        cross_sq = [keep.tile([P, 2, V], F32, name=f"cross_sq{tp}") for tp in range(2)]
+        within = [keep.tile([P, 2, V], F32, name=f"within{tp}", tag=f"within{tp}", align_bytes=64) for tp in range(2)]
+        var = [keep.tile([P, PACK, VH], F32, name=f"var{u}") for u in range(2)]
+        early_bank = []
+
+        def products(t):
             banks = []
             for half in (1, 0):
                 bank = psum.tile([P, HALF], F32, name=f"h{half}{t}", tag=f"h{half}{t}")
-                cols = slice(half * HALF, (half + 1) * HALF)
-                nc.tensor.matmul_mx(out=bank[:], lhsT=w1_codes[:, t, :].bitcast(FP8X4), lhsT_scale=w1_scales[:, t, :],
-                                    rhs=x_codes[:, cols].bitcast(FP8X4), rhs_scale=x_scales[:, cols],
+                nc.tensor.matmul_mx(out=bank[:], lhsT=w1_codes[t][:].bitcast(FP8X4), lhsT_scale=w1_scales[t][:],
+                                    rhs=x_codes[half][:].bitcast(FP8X4), rhs_scale=x_scales[half][:],
                                     start=True, stop=True)
                 banks.append(bank)
             nc.scalar.activation(late[t][:], banks[0][:], ACT.Copy, scale=0.25)
-            nc.vector.scalar_tensor_tensor(sums[:, t, :, :].rearrange("p d v -> p (d v)"), banks[1][:], 0.25, late[t][:],
-                                           ALU.mult, ALU.add)
-            nc.vector.scalar_tensor_tensor(diffs[:, t, :, :].rearrange("p d v -> p (d v)"), banks[1][:], 0.25, late[t][:],
-                                           ALU.mult, ALU.subtract)
-            if t % 2 == 1:
-                nc.scalar.activation(diffs_sq[:, t - 1:t + 1, :, :], diffs[:, t - 1:t + 1, :, :], ACT.Square,
-                                     bias=zero_root[:])
+            early_bank.append(banks[1])
 
-        cross = keep.tile([P, PACK, V], F32, name="cross")
-        nc.vector.tensor_tensor(cross[:], sums[:, :, 0, :], sums[:, :, 1, :], ALU.subtract)
-        cross_sq = keep.tile([P, PACK, V], F32, name="cross_sq")
-        nc.scalar.activation(cross_sq[:], cross[:], ACT.Square)
+        def pair_sums(t):
+            nc.vector.scalar_tensor_tensor(sums[:, t, :, :].rearrange("p d v -> p (d v)"), early_bank[t][:], 0.25,
+                                           late[t][:], ALU.mult, ALU.add)
 
-        mean_bf = keep.tile([P, V, PACK], BF16, name="mean_bf", align_bytes=64)
-        nc.vector.tensor_tensor(mean_bf[:].rearrange("p (c i) t -> p c t i", i=4),
-                                sums[:, :, 0, :].rearrange("p t (c i) -> p c t i", i=4),
-                                sums[:, :, 1, :].rearrange("p t (c i) -> p c t i", i=4), ALU.add)
-        within = keep.tile([P, PACK, V], F32, name="within")
-        nc.vector.tensor_tensor(within[:], diffs_sq[:, :, 0, :], diffs_sq[:, :, 1, :], ALU.add)
-        nc.vector.quantize_mx(out=w23_codes[:].bitcast(FP8X4), scales=w23_scales[:],
-                              in_=w23_bf[:].rearrange("p g n j -> p (g n j)"))
+        def pair_diffs(t):
+            nc.vector.scalar_tensor_tensor(diffs[t][:].rearrange("p d v -> p (d v)"), early_bank[t][:], 0.25,
+                                           late[t][:], ALU.mult, ALU.subtract)
+            nc.scalar.activation(diffs_sq[t][:], diffs[t][:], ACT.Square, bias=zero_root[:])
+
+        def cross_up(t, engine):
+            engine.tensor_tensor(cross[t][:], sums[:, t, 0, :], sums[:, t, 1, :], ALU.subtract)
+            nc.scalar.activation(cross_sq[t // 2][:, t % 2, :], cross[t][:], ACT.Square)
+
+        def within_up(t, engine):
+            engine.tensor_tensor(within[t // 2][:, t % 2, :], diffs_sq[t][:, 0, :], diffs_sq[t][:, 1, :], ALU.add)
+
+        def variance(tp, u):
+            cols = slice(u * VH, (u + 1) * VH)
+            nc.vector.scalar_tensor_tensor(var[u][:, 2 * tp:2 * tp + 2, :], within[tp][:, :, cols], 2.0,
+                                           cross_sq[tp][:, :, cols], ALU.mult, ALU.add)
+
+        for t in range(PACK):
+            products(t)
+        for t in range(PACK - 1):
+            pair_sums(t)
+            pair_diffs(t)
+            cross_up(t, nc.gpsimd)
+            if t == 1:
+                within_up(0, nc.gpsimd)
+        pair_diffs(3)
+        pair_sums(3)
+        within_up(1, nc.vector)
+        cross_up(3, nc.vector)
+        within_up(2, nc.vector)
+        variance(0, 0)
+        within_up(3, nc.vector)
+        variance(0, 1)
+        variance(1, 0)
+        variance(1, 1)
+
         stat_codes = [keep.tile([P, V], U32, name=f"stat_codes{g}", align_bytes=64) for g in range(2)]
         stat_scales = [keep.tile([P, V], U8, name=f"stat_scales{g}", align_bytes=64) for g in range(2)]
-
-        VH = V // 2
-        var = [keep.tile([P, PACK, VH], F32, name=f"var{u}") for u in range(2)]
-        dev_bf = [keep.tile([P, VH, PACK], BF16, name=f"dev_bf{u}", align_bytes=64) for u in range(2)]
+        dev_bf = keep.tile([P, V, PACK], BF16, name="dev_bf", align_bytes=64)
         for u in range(2):
-            cols = slice(u * VH, (u + 1) * VH)
-            nc.vector.scalar_tensor_tensor(var[u][:], within[:, :, cols], 2.0, cross_sq[:, :, cols], ALU.mult, ALU.add)
-            nc.scalar.activation(dev_bf[u][:].rearrange("p (c i) t -> p c t i", i=4),
+            nc.scalar.activation(dev_bf[:, u * VH:(u + 1) * VH, :].rearrange("p (c i) t -> p c t i", i=4),
                                  var[u][:].rearrange("p t (c i) -> p c t i", i=4), ACT.Sqrt)
-        nc.vector.quantize_mx(out=stat_codes[0][:].bitcast(FP8X4), scales=stat_scales[0][:],
-                              in_=mean_bf[:].rearrange("p v t -> p (v t)"))
+        mean_bf = [keep.tile([P, VH, PACK], BF16, name="mean_bf0", align_bytes=64),
+                   keep.tile([P, VH, PACK], BF16, name="mean_bf1", tag="within1", align_bytes=64)]
         for u in range(2):
             cols = slice(u * VH, (u + 1) * VH)
-            nc.vector.quantize_mx(out=stat_codes[1][:, cols].bitcast(FP8X4), scales=stat_scales[1][:, cols],
-                                  in_=dev_bf[u][:].rearrange("p v t -> p (v t)"))
+            nc.vector.tensor_tensor(mean_bf[u][:].rearrange("p (c i) t -> p c t i", i=4),
+                                    sums[:, :, 0, cols].rearrange("p t (c i) -> p c t i", i=4),
+                                    sums[:, :, 1, cols].rearrange("p t (c i) -> p c t i", i=4), ALU.add)
+        w3_bf = keep.tile([P, N, PACK], BF16, name="w3_bf", align_bytes=64)
+        for u in range(2):
+            cols = slice(u * (N // 2), (u + 1) * (N // 2))
+            nc.scalar.copy(w3_bf[:, cols, :].rearrange("p (c i) j -> p c j i", i=4),
+                           w23_raw[1][:, :, cols].rearrange("p j (c i) -> p c j i", i=4))
+        nc.vector.quantize_mx(out=w23_codes[1][:].bitcast(FP8X4), scales=w23_scales[1][:],
+                              in_=w3_bf[:].rearrange("p n j -> p (n j)"))
+        for u in range(2):
+            cols = slice(u * VH, (u + 1) * VH)
+            nc.vector.quantize_mx(out=stat_codes[0][:, cols].bitcast(FP8X4), scales=stat_scales[0][:, cols],
+                                  in_=mean_bf[u][:].rearrange("p v t -> p (v t)"))
+        nc.vector.quantize_mx(out=stat_codes[1][:].bitcast(FP8X4), scales=stat_scales[1][:],
+                              in_=dev_bf[:].rearrange("p v t -> p (v t)"))
 
         acc = psum.tile([P, V], F32, name="acc", tag="h10")
         for g in range(2):
-            cols = slice(g * N, (g + 1) * N)
-            nc.tensor.matmul_mx(out=acc[:], lhsT=w23_codes[:, cols].bitcast(FP8X4), lhsT_scale=w23_scales[:, cols],
+            nc.tensor.matmul_mx(out=acc[:], lhsT=w23_codes[g][:].bitcast(FP8X4), lhsT_scale=w23_scales[g][:],
                                 rhs=stat_codes[g][:].bitcast(FP8X4), rhs_scale=stat_scales[g][:],
                                 start=(g == 0), stop=(g == 1))
         result = keep.tile([P, V], F32, name="result")
-        nc.vector.tensor_copy(result[:], acc[:])
+        nc.scalar.copy(result[:], acc[:])
         nc.sync.dma_start(out=out, in_=result[:])

from contextlib import ExitStack

import concourse.mybir as mybir

K, T, S, V, H, N = 512, 2048, 512, 128, 512, 128
FLOPS = 2 * K * H * S + 2 * 2 * H * N * V

F32 = mybir.dt.float32
BF16 = mybir.dt.bfloat16
U32 = mybir.dt.uint32
U16 = mybir.dt.uint16
U8 = mybir.dt.uint8
FP8X4 = mybir.dt.float8_e4m3fn_x4
ACT = mybir.ActivationFunctionType
ALU = mybir.AluOpType

P = 128
PACK = 4
HALF = S // 2
MH = P // 2


def tile_picked_statpool_none_e_kernel(tc, xT, w1, w2, w3, offs, out):
    nc = tc.nc
    with ExitStack() as ctx:
        keep = ctx.enter_context(tc.tile_pool(name="keep", bufs=1))
        psum = ctx.enter_context(tc.psum_pool(name="psum", bufs=1))

        offsets = keep.tile([P, S // 16], U16, name="offsets")
        x_rows = xT.rearrange("(p j) t -> p j t", j=PACK)
        x_raw = [keep.tile([P, T], F32, name=f"x_raw{j}") for j in range(PACK)]
        nc.sync.dma_start(out=x_raw[0][:], in_=x_rows[:, 0, :])
        nc.sync.dma_start(offsets[:], offs)
        for j in range(1, PACK):
            nc.sync.dma_start(out=x_raw[j][:], in_=x_rows[:, j, :])
        w1_rows = w1.rearrange("(p j) c -> p j c", j=PACK)
        w1_raw = [keep.tile([P, PACK, H // 2], F32, name=f"w1_raw{h}") for h in range(2)]
        for h in range(2):
            nc.sync.dma_start(out=w1_raw[h][:], in_=w1_rows[:, :, h * (H // 2):(h + 1) * (H // 2)])
        w23_raw = [keep.tile([P, PACK, N], F32, name=f"w23_raw{g}") for g in range(2)]
        for g, w in enumerate((w2, w3)):
            nc.sync.dma_start(out=w23_raw[g][:], in_=w.rearrange("(p j) n -> p j n", j=PACK))

        zero = keep.tile([P, 1], F32, name="zero")
        nc.gpsimd.memset(zero[:], 0.0)
        zero_root = keep.tile([P, 1], F32, name="zero_root")
        nc.scalar.activation(zero_root[:], zero[:], ACT.Sqrt)

        x_bf = [keep.tile([P, HALF, PACK], BF16, name=f"x_bf{h}", align_bytes=64) for h in range(2)]
        for j in range(PACK):
            for half in (1, 0):
                nc.vector.tensor_copy(x_bf[half][:, :, j],
                                      x_raw[j][:].indirect(offsets[:, half * (HALF // 16):(half + 1) * (HALF // 16)]))
        x_codes = [keep.tile([P, HALF], U32, name=f"x_codes{h}", align_bytes=64) for h in range(2)]
        x_scales = [keep.tile([P, HALF], U8, name=f"x_scales{h}", align_bytes=64) for h in range(2)]
        for half in (1, 0):
            nc.vector.quantize_mx(out=x_codes[half][:].bitcast(FP8X4), scales=x_scales[half][:],
                                  in_=x_bf[half][:].rearrange("p s j -> p (s j)"))

        w1_codes = [keep.tile([P, P], U32, name=f"w1_codes{t}", align_bytes=64) for t in range(PACK)]
        w1_scales = [keep.tile([P, P], U8, name=f"w1_scales{t}", align_bytes=64) for t in range(PACK)]
        w1_bf = [[keep.tile([P, 2, MH, PACK], BF16, name=f"w1_bf{h}{tp}", tag=f"w1_bf{h}{tp}", align_bytes=64) for tp in range(2)]
                 for h in range(2)]

        def cast_w1(h, tp, on_vector):
            src = w1_raw[h][:].rearrange("p j (m t) -> p m j t", t=PACK)[:, :, :, 2 * tp:2 * tp + 2]
            dst = w1_bf[h][tp][:].rearrange("p t m j -> p m j t")
            if on_vector:
                nc.vector.tensor_copy(dst, src)
            else:
                nc.scalar.copy(dst, src)

        def quant_w1(h, t):
            cols = slice(h * MH, (h + 1) * MH)
            nc.vector.quantize_mx(out=w1_codes[t][:, cols].bitcast(FP8X4), scales=w1_scales[t][:, cols],
                                  in_=w1_bf[h][t // 2][:, t % 2, :, :].rearrange("p m j -> p (m j)"))

        cast_w1(0, 0, False)
        cast_w1(0, 1, False)
        quant_w1(0, 0)
        quant_w1(0, 1)
        quant_w1(0, 2)
        quant_w1(0, 3)
        cast_w1(1, 0, False)
        cast_w1(1, 1, False)
        for t in range(PACK):
            quant_w1(1, t)

        w23_codes = [keep.tile([P, N], U32, name=f"w23_codes{g}", align_bytes=64) for g in range(2)]
        w23_scales = [keep.tile([P, N], U8, name=f"w23_scales{g}", align_bytes=64) for g in range(2)]
        w2_bf = keep.tile([P, N, PACK], BF16, name="w2_bf", tag="w1_bf10", align_bytes=64)
        nc.vector.tensor_copy(w2_bf[:].rearrange("p (c i) j -> p c j i", i=4),
                              w23_raw[0][:].rearrange("p j (c i) -> p c j i", i=4))
        nc.vector.quantize_mx(out=w23_codes[0][:].bitcast(FP8X4), scales=w23_scales[0][:],
                              in_=w2_bf[:].rearrange("p n j -> p (n j)"))

        VH = V // 2
        sums = keep.tile([P, PACK, 2, V], F32, name="sums")
        diffs = [keep.tile([P, 2, V], F32, name=f"diffs{t}") for t in range(PACK)]
        diffs_sq = [keep.tile([P, 2, V], F32, name=f"diffs_sq{t}") for t in range(PACK)]
        late = [keep.tile([P, HALF], F32, name=f"late{t}") for t in range(PACK)]
        cross = [keep.tile([P, V], F32, name=f"cross{t}") for t in range(PACK)]
        cross_sq = [keep.tile([P, 2, V], F32, name=f"cross_sq{tp}") for tp in range(2)]
        within = [keep.tile([P, 2, V], F32, name=f"within{tp}", tag=f"within{tp}", align_bytes=64) for tp in range(2)]
        var = [keep.tile([P, PACK, VH], F32, name=f"var{u}") for u in range(2)]
        early_bank = []

        def products(t):
            banks = []
            for half in (1, 0):
                bank = psum.tile([P, HALF], F32, name=f"h{half}{t}", tag=f"h{half}{t}")
                nc.tensor.matmul_mx(out=bank[:], lhsT=w1_codes[t][:].bitcast(FP8X4), lhsT_scale=w1_scales[t][:],
                                    rhs=x_codes[half][:].bitcast(FP8X4), rhs_scale=x_scales[half][:],
                                    start=True, stop=True)
                banks.append(bank)
            nc.scalar.activation(late[t][:], banks[0][:], ACT.Copy, scale=0.25)
            early_bank.append(banks[1])

        def pair_sums(t):
            nc.vector.scalar_tensor_tensor(sums[:, t, :, :].rearrange("p d v -> p (d v)"), early_bank[t][:], 0.25,
                                           late[t][:], ALU.mult, ALU.add)

        def pair_diffs(t):
            nc.vector.scalar_tensor_tensor(diffs[t][:].rearrange("p d v -> p (d v)"), early_bank[t][:], 0.25,
                                           late[t][:], ALU.mult, ALU.subtract)
            nc.scalar.activation(diffs_sq[t][:], diffs[t][:], ACT.Square, bias=zero_root[:])

        def cross_up(t, engine):
            engine.tensor_tensor(cross[t][:], sums[:, t, 0, :], sums[:, t, 1, :], ALU.subtract)
            nc.scalar.activation(cross_sq[t // 2][:, t % 2, :], cross[t][:], ACT.Square)

        def within_up(t, engine):
            engine.tensor_tensor(within[t // 2][:, t % 2, :], diffs_sq[t][:, 0, :], diffs_sq[t][:, 1, :], ALU.add)

        def variance(tp, u):
            cols = slice(u * VH, (u + 1) * VH)
            nc.vector.scalar_tensor_tensor(var[u][:, 2 * tp:2 * tp + 2, :], within[tp][:, :, cols], 2.0,
                                           cross_sq[tp][:, :, cols], ALU.mult, ALU.add)

        for t in range(PACK):
            products(t)
        for t in range(PACK - 1):
            pair_sums(t)
            pair_diffs(t)
            cross_up(t, nc.gpsimd)
            if t == 1:
                within_up(0, nc.gpsimd)
        pair_diffs(3)
        pair_sums(3)
        within_up(1, nc.vector)
        cross_up(3, nc.vector)
        within_up(2, nc.vector)
        variance(0, 0)
        within_up(3, nc.vector)
        variance(0, 1)
        variance(1, 0)
        variance(1, 1)

        stat_codes = [keep.tile([P, V], U32, name=f"stat_codes{g}", align_bytes=64) for g in range(2)]
        stat_scales = [keep.tile([P, V], U8, name=f"stat_scales{g}", align_bytes=64) for g in range(2)]
        dev_bf = keep.tile([P, V, PACK], BF16, name="dev_bf", align_bytes=64)
        for u in range(2):
            nc.scalar.activation(dev_bf[:, u * VH:(u + 1) * VH, :].rearrange("p (c i) t -> p c t i", i=4),
                                 var[u][:].rearrange("p t (c i) -> p c t i", i=4), ACT.Sqrt)
        mean_bf = [keep.tile([P, VH, PACK], BF16, name="mean_bf0", align_bytes=64),
                   keep.tile([P, VH, PACK], BF16, name="mean_bf1", tag="within1", align_bytes=64)]
        for u in range(2):
            cols = slice(u * VH, (u + 1) * VH)
            nc.vector.tensor_tensor(mean_bf[u][:].rearrange("p (c i) t -> p c t i", i=4),
                                    sums[:, :, 0, cols].rearrange("p t (c i) -> p c t i", i=4),
                                    sums[:, :, 1, cols].rearrange("p t (c i) -> p c t i", i=4), ALU.add)
        w3_bf = keep.tile([P, N, PACK], BF16, name="w3_bf", align_bytes=64)
        for u in range(2):
            cols = slice(u * (N // 2), (u + 1) * (N // 2))
            nc.scalar.copy(w3_bf[:, cols, :].rearrange("p (c i) j -> p c j i", i=4),
                           w23_raw[1][:, :, cols].rearrange("p j (c i) -> p c j i", i=4))
        nc.vector.quantize_mx(out=w23_codes[1][:].bitcast(FP8X4), scales=w23_scales[1][:],
                              in_=w3_bf[:].rearrange("p n j -> p (n j)"))
        for u in range(2):
            cols = slice(u * VH, (u + 1) * VH)
            nc.vector.quantize_mx(out=stat_codes[0][:, cols].bitcast(FP8X4), scales=stat_scales[0][:, cols],
                                  in_=mean_bf[u][:].rearrange("p v t -> p (v t)"))
        nc.vector.quantize_mx(out=stat_codes[1][:].bitcast(FP8X4), scales=stat_scales[1][:],
                              in_=dev_bf[:].rearrange("p v t -> p (v t)"))

        acc = psum.tile([P, V], F32, name="acc", tag="h10")
        for g in range(2):
            nc.tensor.matmul_mx(out=acc[:], lhsT=w23_codes[g][:].bitcast(FP8X4), lhsT_scale=w23_scales[g][:],
                                rhs=stat_codes[g][:].bitcast(FP8X4), rhs_scale=stat_scales[g][:],
                                start=(g == 0), stop=(g == 1))
        result = keep.tile([P, V], F32, name="result")
        nc.scalar.copy(result[:], acc[:])
        nc.sync.dma_start(out=out, in_=result[:])
